import numpy as np
import ml_dtypes


def mxq(x, axis, fmt="e4m3"):
    dtype, down = {"e4m3": (ml_dtypes.float8_e4m3fn, 7), "e5m2": (ml_dtypes.float8_e5m2, 14)}[fmt]
    v = np.moveaxis(np.asarray(x, np.float32).astype(ml_dtypes.bfloat16).astype(np.float64), axis, -1)
    blocks = v.reshape(v.shape[:-1] + (-1, 32))
    amax = np.abs(blocks).max(-1, keepdims=True)
    byte = np.maximum(np.where(amax > 0, np.frexp(amax)[1] - 1 + 127, 0) - down, 1)
    scale = np.exp2(byte - 127.0)
    codes = (blocks / scale).astype(np.float32).astype(dtype).astype(np.float64)
    return np.moveaxis((codes * scale).reshape(v.shape), -1, axis)


WIDE = False


def mx_kscale(k):
    if not WIDE:
        return np.ones(k)
    levels = np.array([10, -10, 5, -5, 0])
    if k % 512:
        return np.exp2(np.random.permutation(np.resize(levels, k // 32))).repeat(32)
    a = np.empty((k // 512, 16))
    for p in range(k // 512):
        a[p, :8] = np.random.permutation(np.resize(levels, 8))
        for g in range(8):
            far = levels[np.abs(levels - a[p, g]) >= 10]
            a[p, g + 8] = far[np.random.randint(len(far))]
    return np.exp2(a.ravel()).repeat(32)


def f64(x):
    return np.asarray(x).astype(np.float64)


def striped8(idx):
    return np.asarray(idx).reshape(8, -1, 16).transpose(0, 2, 1).reshape(128, -1).astype(np.uint16)


def unstriped8(offs):
    return offs.reshape(8, 16, -1).transpose(0, 2, 1).reshape(8, -1).astype(np.int64)


def pick8(x, idx, run):
    r = np.arange(len(x))
    return x[r[:, None], idx[r % (8 * run) // run]]


E2M1 = np.array([0.0, 0.5, 1.0, 1.5, 2.0, 3.0, 4.0, 6.0, -0.0, -0.5, -1.0, -1.5, -2.0, -3.0, -4.0, -6.0])


def pack_weight(w, fmt):
    k, n = w.shape
    w = f64(np.asarray(w, np.float32).astype(ml_dtypes.bfloat16)).reshape(k // 32, 32, n)
    amax = np.abs(w).max(1)
    if fmt == "e4m3":
        byte = np.frexp(amax)[1] - 1 + 127 - 7
    else:
        mant, ex = np.frexp(amax / 6.0)
        byte = np.where(mant > 0.5, ex, ex - 1) + 127
    byte = np.clip(np.where(amax > 0, byte, 1), 1, 254)
    scaled = (w * np.exp2(127.0 - byte)[:, None, :]).reshape(k, n).astype(np.float32)
    by_word = np.ascontiguousarray(scaled.reshape(k // 512, 128, 4, n).transpose(0, 1, 3, 2))
    if fmt == "e4m3":
        words = by_word.astype(ml_dtypes.float8_e4m3fn).view(np.uint8)
    else:
        c = by_word.astype(ml_dtypes.float4_e2m1fn).view(np.uint8) & 0xF
        words = (c[..., 0::2] | (c[..., 1::2] << 4)).reshape(k // 512, 128, 2 * n)
    return np.ascontiguousarray(words), np.ascontiguousarray(byte.astype(np.uint8).reshape(k // 512, 16, n))


def unpack_weight(words, scales, fmt):
    g, _, n = scales.shape
    words = np.ascontiguousarray(words).reshape(g, 128, n, -1)
    if fmt == "e4m3":
        vals = words.view(ml_dtypes.float8_e4m3fn).astype(np.float64)
    else:
        nib = np.empty((g, 128, n, 4), np.uint8)
        nib[..., 0::2] = words & 0xF
        nib[..., 1::2] = words >> 4
        vals = E2M1[nib]
    vals = vals * np.repeat(np.exp2(scales.astype(np.float64) - 127.0), 8, axis=1)[..., None]
    return vals.transpose(0, 1, 3, 2).reshape(g * 512, n)


def sigmoid(v):
    return 1.0 / (1.0 + np.exp(-v))


D, T, I, Q = 512, 1024, 512, 128


def setup_inputs():
    n = np.random.standard_normal
    idx = np.stack([np.random.permutation(T)[:I] for _ in range(8)])
    idx2 = np.stack([np.random.permutation(T)[:I] for _ in range(8)])
    idx3 = np.stack([np.random.permutation(T)[:I] for _ in range(8)])
    idx4 = np.stack([np.random.permutation(T)[:I] for _ in range(8)])
    fd = mx_kscale(D)
    keysp = pack_weight(n((D, T)) / fd[:, None], "e2m1")
    return {
        "query": (n((D, Q)) * 0.9 / np.sqrt(D) * fd[:, None]).astype(np.float32),
        "keys_words": keysp[0],
        "keys_scales": keysp[1],
        "lam": (np.random.uniform(0.3, 0.9, (Q, 1))).astype(np.float32),
        "old": (1.0 * n((Q, T))).astype(np.float32),
        "share2": (np.random.uniform(0.4, 1.2, (Q, 1))).astype(np.float32),
        "offs": striped8(idx),
        "offs2": striped8(idx2),
        "offs3": striped8(idx3),
        "offs4": striped8(idx4),
    }


def reference(query, keys_words, keys_scales, lam, old, share2, offs, offs2, offs3, offs4):
    idx = unstriped8(offs)
    idx2 = unstriped8(offs2)
    idx3 = unstriped8(offs3)
    idx4 = unstriped8(offs4)
    keysu = unpack_weight(keys_words, keys_scales, "e2m1")
    queryq = mxq(f64(query), 0, "e4m3")
    a = queryq.T @ keysu
    s = pick8(a, idx, 16) + np.maximum(pick8(a, idx2, 16), pick8(a, idx3, 16)) * f64(lam)
    w = sigmoid(s)
    f1 = np.zeros((Q, T))
    f1[np.arange(Q)[:, None], idx[np.arange(Q) % 128 // 16]] = w
    f2 = np.zeros((Q, T))
    f2[np.arange(Q)[:, None], idx4[np.arange(Q) % 128 // 16]] = w
    y = f64(old) + f1 + f2 * f64(share2)
    return y

@@ -1,0 +1,128 @@
+from contextlib import ExitStack
+
+import concourse.mybir as mybir
+
+D, T, I, Q = 512, 1024, 512, 128
+FLOPS = 2 * D * T * Q
+
+F32 = mybir.dt.float32
+BF16 = mybir.dt.bfloat16
+I32 = mybir.dt.int32
+U32 = mybir.dt.uint32
+U16 = mybir.dt.uint16
+U8 = mybir.dt.uint8
+FP8X4 = mybir.dt.float8_e4m3fn_x4
+FP4X4 = mybir.dt.float4_e2m1fn_x4
+ALU = mybir.AluOpType
+ACT = mybir.ActivationFunctionType
+
+P = 128
+PACK = 4
+GROUP = 16
+MM_WIDTHS = (256, 256, 256, 128, 128)
+HALF = I // 2
+N_OUT = 256
+LEAD = 128
+
+
+def tile_attend_lookahead_lean_twiceput_heads_kernel(
+    tc, query, keys_words, keys_scales, lam, old, share2, offs, offs2, offs3, offs4, out
+):
+    nc = tc.nc
+    with ExitStack() as ctx:
+        lists = ctx.enter_context(tc.tile_pool(name="lists", bufs=1))
+        keep = ctx.enter_context(tc.tile_pool(name="keep", bufs=1))
+        psum = ctx.enter_context(tc.psum_pool(name="psum", bufs=1))
+
+        q_raw = keep.tile([P, PACK, Q], F32, name="q_raw")
+        nc.sync.dma_start(out=q_raw[:], in_=query.rearrange("(p j) q -> p j q", j=PACK))
+        k_words = keep.tile([P, 2 * T], U8, name="k_words", align_bytes=64)
+        nc.sync.dma_start(out=k_words[:].bitcast(I32), in_=keys_words[0].bitcast(I32))
+        k_scales = keep.tile([P, T], U8, name="k_scales", align_bytes=64)
+        for quad in range(4):
+            nc.sync.dma_start(
+                out=k_scales[32 * quad : 32 * quad + 4, :].bitcast(I32),
+                in_=keys_scales[0, 4 * quad : 4 * quad + 4, :].bitcast(I32),
+            )
+        list2 = lists.tile([P, I // GROUP], U16, name="list2")
+        nc.sync.dma_start(list2[:], offs2)
+        list3 = lists.tile([P, I // GROUP], U16, name="list3")
+        nc.sync.dma_start(list3[:], offs3)
+        list1 = lists.tile([P, I // GROUP], U16, name="list1")
+        nc.sync.dma_start(list1[:], offs)
+        lam_sb = keep.tile([P, 1], F32, name="lam_sb")
+        nc.sync.dma_start(out=lam_sb[:], in_=lam)
+        list4 = lists.tile([P, I // GROUP], U16, name="list4")
+        nc.sync.dma_start(list4[:], offs4)
+        old_sb = keep.tile([P, T], F32, name="old_sb")
+        nc.sync.dma_start(out=old_sb[:], in_=old)
+        share_sb = keep.tile([P, 1], F32, name="share_sb")
+        nc.sync.dma_start(out=share_sb[:], in_=share2)
+
+        f1 = keep.tile([P, T], F32, name="f1")
+        f2 = keep.tile([P, T], F32, name="f2")
+        nc.vector.memset(f1[:], 0.0)
+        nc.vector.memset(f2[:], 0.0)
+
+        q_bf = keep.tile([P, Q, PACK], BF16, name="q_bf", align_bytes=64)
+        nc.vector.tensor_copy(
+            out=q_bf[:].rearrange("p (c i) j -> p c j i", i=4),
+            in_=q_raw[:].rearrange("p j (c i) -> p c j i", i=4),
+        )
+        q_codes = keep.tile([P, Q], U32, name="q_codes", align_bytes=64)
+        q_scales = keep.tile([P, Q], U8, name="q_scales", align_bytes=64)
+        nc.vector.quantize_mx(
+            out=q_codes[:].bitcast(FP8X4), scales=q_scales[:], in_=q_bf[:].rearrange("p q j -> p (q j)")
+        )
+
+        a = keep.tile([P, T], F32, name="a")
+        for n, width in enumerate(MM_WIDTHS):
+            first = sum(MM_WIDTHS[:n])
+            cols = slice(first, first + width)
+            acc = psum.tile([P, width], F32, name="acc%d" % n)
+            nc.tensor.matmul_mx(
+                out=acc[:],
+                lhsT=q_codes[:].bitcast(FP8X4),
+                lhsT_scale=q_scales[:],
+                rhs=k_words[:, 2 * first : 2 * (first + width)].bitcast(FP4X4),
+                rhs_scale=k_scales[:, cols],
+                start=True,
+                stop=True,
+            )
+            if n % 2 == 0:
+                nc.vector.tensor_copy(out=a[:, cols], in_=acc[:])
+            else:
+                nc.scalar.copy(out=a[:, cols], in_=acc[:])
+
+        w = keep.tile([P, I], F32, name="w")
+        for h in range(2):
+            entries = slice(h * HALF // GROUP, (h + 1) * HALF // GROUP)
+            slots = slice(h * HALF, (h + 1) * HALF)
+            g2 = keep.tile([P, HALF], F32, name="g2_%d" % h)
+            nc.scalar.activation(g2[:], a[:].indirect(list2[:, entries]), ACT.Copy)
+            g3 = keep.tile([P, HALF], F32, name="g3_%d" % h)
+            nc.vector.tensor_copy(g3[:], a[:].indirect(list3[:, entries]))
+            g1 = keep.tile([P, HALF], F32, name="g1_%d" % h)
+            nc.scalar.activation(g1[:], a[:].indirect(list1[:, entries]), ACT.Copy)
+            larger = keep.tile([P, HALF], F32, name="larger%d" % h)
+            nc.vector.tensor_tensor(larger[:], g2[:], g3[:], ALU.max)
+            s = keep.tile([P, HALF], F32, name="s%d" % h)
+            nc.vector.scalar_tensor_tensor(s[:], larger[:], lam_sb[:], g1[:], ALU.mult, ALU.add)
+            if h == 0:
+                nc.scalar.activation(w[:, :LEAD], s[:, :LEAD], ACT.Sigmoid)
+                nc.scalar.activation(w[:, LEAD:HALF], s[:, LEAD:], ACT.Sigmoid)
+            else:
+                nc.scalar.activation(w[:, slots], s[:], ACT.Sigmoid)
+
+        nc.vector.tensor_copy(f2[:].indirect(list4[:, : LEAD // GROUP]), w[:, :LEAD])
+        nc.vector.tensor_copy(f1[:].indirect(list1[:]), w[:])
+        nc.vector.tensor_copy(f2[:].indirect(list4[:, LEAD // GROUP :]), w[:, LEAD:])
+
+        for n in range(T // N_OUT):
+            cols = slice(n * N_OUT, (n + 1) * N_OUT)
+            part = keep.tile([P, N_OUT], F32, name="part%d" % n)
+            nc.gpsimd.tensor_tensor(part[:], old_sb[:, cols], f1[:, cols], ALU.add)
+            res = keep.tile([P, N_OUT], F32, name="res%d" % n)
+            nc.vector.scalar_tensor_tensor(res[:], f2[:, cols], share_sb[:], part[:], ALU.mult, ALU.add)
+            queue = nc.sync if n % 2 == 0 else nc.scalar
+            queue.dma_start(out=out[:, cols], in_=res[:])

@@ -34,6 +34,11 @@ def tile_attend_lookahead_lean_twiceput_heads_kernel(
         keep = ctx.enter_context(tc.tile_pool(name="keep", bufs=1))
         psum = ctx.enter_context(tc.psum_pool(name="psum", bufs=1))
 
+        warm_in = keep.tile([P, 1], F32, name="warm_in")
+        warm_out = keep.tile([P, 1], F32, name="warm_out")
+        nc.gpsimd.memset(warm_in[:], 0.0)
+        nc.scalar.activation(warm_out[:], warm_in[:], ACT.Sigmoid)
+
         q_raw = keep.tile([P, PACK, Q], F32, name="q_raw")
         nc.sync.dma_start(out=q_raw[:], in_=query.rearrange("(p j) q -> p j q", j=PACK))
         k_words = keep.tile([P, 2 * T], U8, name="k_words", align_bytes=64)

@@ -1,6 +1,7 @@
 from contextlib import ExitStack
 
 import concourse.mybir as mybir
+from concourse.masks import make_identity
 
 D, T, I, Q = 512, 1024, 512, 128
 FLOPS = 2 * D * T * Q
@@ -64,6 +65,9 @@ def tile_attend_lookahead_lean_twiceput_heads_kernel(
         share_sb = keep.tile([P, 1], F32, name="share_sb")
         nc.sync.dma_start(out=share_sb[:], in_=share2)
 
+        ident = keep.tile([P, P], F32, name="ident")
+        make_identity(nc, ident[:])
+
         f1 = keep.tile([P, T], F32, name="f1")
         f2 = keep.tile([P, T], F32, name="f2")
         nc.vector.memset(f1[:], 0.0)
@@ -84,7 +88,7 @@ def tile_attend_lookahead_lean_twiceput_heads_kernel(
         for n, width in enumerate(MM_WIDTHS):
             first = sum(MM_WIDTHS[:n])
             cols = slice(first, first + width)
-            acc = psum.tile([P, width], F32, name="acc%d" % n)
+            acc = psum.tile([P, width], F32, name="acc%d" % n, tag="bank%d" % n)
             nc.tensor.matmul_mx(
                 out=acc[:],
                 lhsT=q_codes[:].bitcast(FP8X4),
@@ -99,34 +103,65 @@ def tile_attend_lookahead_lean_twiceput_heads_kernel(
             else:
                 nc.scalar.copy(out=a[:, cols], in_=acc[:])
 
-        w = keep.tile([P, I], F32, name="w")
-        for h in range(2):
-            entries = slice(h * HALF // GROUP, (h + 1) * HALF // GROUP)
-            slots = slice(h * HALF, (h + 1) * HALF)
-            g2 = keep.tile([P, HALF], F32, name="g2_%d" % h)
-            nc.scalar.activation(g2[:], a[:].indirect(list2[:, entries]), ACT.Copy)
-            g3 = keep.tile([P, HALF], F32, name="g3_%d" % h)
-            nc.vector.tensor_copy(g3[:], a[:].indirect(list3[:, entries]))
-            g1 = keep.tile([P, HALF], F32, name="g1_%d" % h)
-            nc.scalar.activation(g1[:], a[:].indirect(list1[:, entries]), ACT.Copy)
-            larger = keep.tile([P, HALF], F32, name="larger%d" % h)
-            nc.vector.tensor_tensor(larger[:], g2[:], g3[:], ALU.max)
-            s = keep.tile([P, HALF], F32, name="s%d" % h)
-            nc.vector.scalar_tensor_tensor(s[:], larger[:], lam_sb[:], g1[:], ALU.mult, ALU.add)
-            if h == 0:
-                nc.scalar.activation(w[:, :LEAD], s[:, :LEAD], ACT.Sigmoid)
-                nc.scalar.activation(w[:, LEAD:HALF], s[:, LEAD:], ACT.Sigmoid)
-            else:
-                nc.scalar.activation(w[:, slots], s[:], ACT.Sigmoid)
+        turned = []
+        for n in range(T // N_OUT):
+            bank = psum.tile([P, N_OUT], F32, name="turned%d" % n, tag="bank%d" % n)
+            turned.append(bank)
+            for b in range(N_OUT // P):
+                nc.tensor.matmul(
+                    bank[:, b * P : (b + 1) * P],
+                    lhsT=old_sb[:, n * N_OUT + b * P : n * N_OUT + (b + 1) * P],
+                    rhs=ident[:],
+                    is_transpose=True,
+                    start=(b == 0),
+                    stop=False,
+                )
 
-        nc.vector.tensor_copy(f2[:].indirect(list4[:, : LEAD // GROUP]), w[:, :LEAD])
-        nc.vector.tensor_copy(f1[:].indirect(list1[:]), w[:])
-        nc.vector.tensor_copy(f2[:].indirect(list4[:, LEAD // GROUP :]), w[:, LEAD:])
+        halves = [slice(h * HALF, (h + 1) * HALF) for h in range(2)]
+        g1 = keep.tile([P, I], F32, name="g1")
+        g2 = keep.tile([P, I], F32, name="g2")
+        g3 = keep.tile([P, I], F32, name="g3")
+        for slots in halves:
+            entries = slice(slots.start // GROUP, slots.stop // GROUP)
+            nc.scalar.activation(g2[:, slots], a[:].indirect(list2[:, entries]), ACT.Copy)
+            nc.scalar.activation(g1[:, slots], a[:].indirect(list1[:, entries]), ACT.Copy)
+            nc.vector.tensor_copy(g3[:, slots], a[:].indirect(list3[:, entries]))
+        larger = keep.tile([P, I], F32, name="larger")
+        s = keep.tile([P, I], F32, name="s")
+        for slots in halves:
+            nc.vector.tensor_tensor(larger[:, slots], g2[:, slots], g3[:, slots], ALU.max)
+            nc.vector.scalar_tensor_tensor(
+                s[:, slots], larger[:, slots], lam_sb[:], g1[:, slots], ALU.mult, ALU.add
+            )
+        w = keep.tile([P, I], F32, name="w")
+        for slots in (slice(0, LEAD), slice(LEAD, HALF), slice(HALF, I)):
+            nc.scalar.activation(w[:, slots], s[:, slots], ACT.Sigmoid)
+
+        for slots in (slice(0, LEAD), slice(LEAD, I)):
+            entries = slice(slots.start // GROUP, slots.stop // GROUP)
+            nc.vector.tensor_copy(f1[:].indirect(list1[:, entries]), w[:, slots])
+            nc.vector.tensor_copy(f2[:].indirect(list4[:, entries]), w[:, slots])
+
+        turned_sb = []
+        for n in range(T // N_OUT):
+            for b in range(N_OUT // P):
+                nc.tensor.matmul(
+                    turned[n][:, b * P : (b + 1) * P],
+                    lhsT=f1[:, n * N_OUT + b * P : n * N_OUT + (b + 1) * P],
+                    rhs=ident[:],
+                    is_transpose=True,
+                    start=False,
+                    stop=(b == N_OUT // P - 1),
+                )
+            moved = keep.tile([P, N_OUT], F32, name="moved%d" % n)
+            nc.scalar.copy(out=moved[:], in_=turned[n][:])
+            turned_sb.append(moved)
 
         for n in range(T // N_OUT):
             cols = slice(n * N_OUT, (n + 1) * N_OUT)
-            part = keep.tile([P, N_OUT], F32, name="part%d" % n)
-            nc.gpsimd.tensor_tensor(part[:], old_sb[:, cols], f1[:, cols], ALU.add)
+            part = psum.tile([P, N_OUT], F32, name="part%d" % n, tag="bank%d" % (4 + n))
+            for b in range(N_OUT // P):
+                nc.tensor.transpose(part[:, b * P : (b + 1) * P], turned_sb[n][:, b * P : (b + 1) * P], ident[:])
             res = keep.tile([P, N_OUT], F32, name="res%d" % n)
             nc.vector.scalar_tensor_tensor(res[:], f2[:, cols], share_sb[:], part[:], ALU.mult, ALU.add)
             queue = nc.sync if n % 2 == 0 else nc.scalar

@@ -42,13 +42,16 @@ def tile_attend_lookahead_lean_twiceput_heads_kernel(
 
         q_raw = keep.tile([P, PACK, Q], F32, name="q_raw")
         nc.sync.dma_start(out=q_raw[:], in_=query.rearrange("(p j) q -> p j q", j=PACK))
-        k_words = keep.tile([P, 2 * T], U8, name="k_words", align_bytes=64)
-        nc.sync.dma_start(out=k_words[:].bitcast(I32), in_=keys_words[0].bitcast(I32))
         k_scales = keep.tile([P, T], U8, name="k_scales", align_bytes=64)
-        for quad in range(4):
+        for r in range(4):
             nc.sync.dma_start(
-                out=k_scales[32 * quad : 32 * quad + 4, :].bitcast(I32),
-                in_=keys_scales[0, 4 * quad : 4 * quad + 4, :].bitcast(I32),
+                out=k_scales[r:P:32, :].bitcast(I32), in_=keys_scales[0, r:16:4, :].bitcast(I32)
+            )
+        k_words = keep.tile([P, 2 * T], U8, name="k_words", align_bytes=64)
+        for h in range(2):
+            nc.sync.dma_start(
+                out=k_words[:, h * T : (h + 1) * T].bitcast(I32),
+                in_=keys_words[0, :, h * T : (h + 1) * T].bitcast(I32),
             )
         list2 = lists.tile([P, I // GROUP], U16, name="list2")
         nc.sync.dma_start(list2[:], offs2)
@@ -65,15 +68,12 @@ def tile_attend_lookahead_lean_twiceput_heads_kernel(
         share_sb = keep.tile([P, 1], F32, name="share_sb")
         nc.sync.dma_start(out=share_sb[:], in_=share2)
 
-        ident = keep.tile([P, P], F32, name="ident")
-        make_identity(nc, ident[:])
-
         f1 = keep.tile([P, T], F32, name="f1")
         f2 = keep.tile([P, T], F32, name="f2")
         nc.vector.memset(f1[:], 0.0)
-        nc.vector.memset(f2[:], 0.0)
+        nc.gpsimd.memset(f2[:], 0.0)
 
-        q_bf = keep.tile([P, Q, PACK], BF16, name="q_bf", align_bytes=64)
+        q_bf = keep.tile([P, Q, PACK], BF16, name="q_bf", tag="q_bf_then_ident", align_bytes=64)
         nc.vector.tensor_copy(
             out=q_bf[:].rearrange("p (c i) j -> p c j i", i=4),
             in_=q_raw[:].rearrange("p j (c i) -> p c j i", i=4),
@@ -83,6 +83,9 @@ def tile_attend_lookahead_lean_twiceput_heads_kernel(
         nc.vector.quantize_mx(
             out=q_codes[:].bitcast(FP8X4), scales=q_scales[:], in_=q_bf[:].rearrange("p q j -> p (q j)")
         )
+
+        ident = keep.tile([P, P], F32, name="ident", tag="q_bf_then_ident", align_bytes=64)
+        make_identity(nc, ident[:])
 
         a = keep.tile([P, T], F32, name="a")
         for n, width in enumerate(MM_WIDTHS):

from contextlib import ExitStack

import concourse.mybir as mybir
from concourse.masks import make_identity

D, T, I, Q = 512, 1024, 512, 128
FLOPS = 2 * D * T * Q

F32 = mybir.dt.float32
BF16 = mybir.dt.bfloat16
I32 = mybir.dt.int32
U32 = mybir.dt.uint32
U16 = mybir.dt.uint16
U8 = mybir.dt.uint8
FP8X4 = mybir.dt.float8_e4m3fn_x4
FP4X4 = mybir.dt.float4_e2m1fn_x4
ALU = mybir.AluOpType
ACT = mybir.ActivationFunctionType

P = 128
PACK = 4
GROUP = 16
MM_WIDTHS = (256, 256, 256, 128, 128)
HALF = I // 2
N_OUT = 256
LEAD = 128


def tile_attend_lookahead_lean_twiceput_heads_kernel(
    tc, query, keys_words, keys_scales, lam, old, share2, offs, offs2, offs3, offs4, out
):
    nc = tc.nc
    with ExitStack() as ctx:
        lists = ctx.enter_context(tc.tile_pool(name="lists", bufs=1))
        keep = ctx.enter_context(tc.tile_pool(name="keep", bufs=1))
        psum = ctx.enter_context(tc.psum_pool(name="psum", bufs=1))

        warm_in = keep.tile([P, 1], F32, name="warm_in")
        warm_out = keep.tile([P, 1], F32, name="warm_out")
        nc.gpsimd.memset(warm_in[:], 0.0)
        nc.scalar.activation(warm_out[:], warm_in[:], ACT.Sigmoid)

        q_raw = keep.tile([P, PACK, Q], F32, name="q_raw")
        nc.sync.dma_start(out=q_raw[:], in_=query.rearrange("(p j) q -> p j q", j=PACK))
        k_scales = keep.tile([P, T], U8, name="k_scales", align_bytes=64)
        for r in range(4):
            nc.sync.dma_start(
                out=k_scales[r:P:32, :].bitcast(I32), in_=keys_scales[0, r:16:4, :].bitcast(I32)
            )
        k_words = keep.tile([P, 2 * T], U8, name="k_words", align_bytes=64)
        for h in range(2):
            nc.sync.dma_start(
                out=k_words[:, h * T : (h + 1) * T].bitcast(I32),
                in_=keys_words[0, :, h * T : (h + 1) * T].bitcast(I32),
            )
        list2 = lists.tile([P, I // GROUP], U16, name="list2")
        nc.sync.dma_start(list2[:], offs2)
        list3 = lists.tile([P, I // GROUP], U16, name="list3")
        nc.sync.dma_start(list3[:], offs3)
        list1 = lists.tile([P, I // GROUP], U16, name="list1")
        nc.sync.dma_start(list1[:], offs)
        lam_sb = keep.tile([P, 1], F32, name="lam_sb")
        nc.sync.dma_start(out=lam_sb[:], in_=lam)
        list4 = lists.tile([P, I // GROUP], U16, name="list4")
        nc.sync.dma_start(list4[:], offs4)
        old_sb = keep.tile([P, T], F32, name="old_sb")
        nc.sync.dma_start(out=old_sb[:], in_=old)
        share_sb = keep.tile([P, 1], F32, name="share_sb")
        nc.sync.dma_start(out=share_sb[:], in_=share2)

        f1 = keep.tile([P, T], F32, name="f1")
        f2 = keep.tile([P, T], F32, name="f2")
        nc.vector.memset(f1[:], 0.0)
        nc.gpsimd.memset(f2[:], 0.0)

        q_bf = keep.tile([P, Q, PACK], BF16, name="q_bf", tag="q_bf_then_ident", align_bytes=64)
        nc.vector.tensor_copy(
            out=q_bf[:].rearrange("p (c i) j -> p c j i", i=4),
            in_=q_raw[:].rearrange("p j (c i) -> p c j i", i=4),
        )
        q_codes = keep.tile([P, Q], U32, name="q_codes", align_bytes=64)
        q_scales = keep.tile([P, Q], U8, name="q_scales", align_bytes=64)
        nc.vector.quantize_mx(
            out=q_codes[:].bitcast(FP8X4), scales=q_scales[:], in_=q_bf[:].rearrange("p q j -> p (q j)")
        )

        ident = keep.tile([P, P], F32, name="ident", tag="q_bf_then_ident", align_bytes=64)
        make_identity(nc, ident[:])

        a = keep.tile([P, T], F32, name="a")
        for n, width in enumerate(MM_WIDTHS):
            first = sum(MM_WIDTHS[:n])
            cols = slice(first, first + width)
            acc = psum.tile([P, width], F32, name="acc%d" % n, tag="bank%d" % n)
            nc.tensor.matmul_mx(
                out=acc[:],
                lhsT=q_codes[:].bitcast(FP8X4),
                lhsT_scale=q_scales[:],
                rhs=k_words[:, 2 * first : 2 * (first + width)].bitcast(FP4X4),
                rhs_scale=k_scales[:, cols],
                start=True,
                stop=True,
            )
            if n % 2 == 0:
                nc.vector.tensor_copy(out=a[:, cols], in_=acc[:])
            else:
                nc.scalar.copy(out=a[:, cols], in_=acc[:])

        turned = []
        for n in range(T // N_OUT):
            bank = psum.tile([P, N_OUT], F32, name="turned%d" % n, tag="bank%d" % n)
            turned.append(bank)
            for b in range(N_OUT // P):
                nc.tensor.matmul(
                    bank[:, b * P : (b + 1) * P],
                    lhsT=old_sb[:, n * N_OUT + b * P : n * N_OUT + (b + 1) * P],
                    rhs=ident[:],
                    is_transpose=True,
                    start=(b == 0),
                    stop=False,
                )

        halves = [slice(h * HALF, (h + 1) * HALF) for h in range(2)]
        g1 = keep.tile([P, I], F32, name="g1")
        g2 = keep.tile([P, I], F32, name="g2")
        g3 = keep.tile([P, I], F32, name="g3")
        for slots in halves:
            entries = slice(slots.start // GROUP, slots.stop // GROUP)
            nc.scalar.activation(g2[:, slots], a[:].indirect(list2[:, entries]), ACT.Copy)
            nc.scalar.activation(g1[:, slots], a[:].indirect(list1[:, entries]), ACT.Copy)
            nc.vector.tensor_copy(g3[:, slots], a[:].indirect(list3[:, entries]))
        larger = keep.tile([P, I], F32, name="larger")
        s = keep.tile([P, I], F32, name="s")
        for slots in halves:
            nc.vector.tensor_tensor(larger[:, slots], g2[:, slots], g3[:, slots], ALU.max)
            nc.vector.scalar_tensor_tensor(
                s[:, slots], larger[:, slots], lam_sb[:], g1[:, slots], ALU.mult, ALU.add
            )
        w = keep.tile([P, I], F32, name="w")
        for slots in (slice(0, LEAD), slice(LEAD, HALF), slice(HALF, I)):
            nc.scalar.activation(w[:, slots], s[:, slots], ACT.Sigmoid)

        for slots in (slice(0, LEAD), slice(LEAD, I)):
            entries = slice(slots.start // GROUP, slots.stop // GROUP)
            nc.vector.tensor_copy(f1[:].indirect(list1[:, entries]), w[:, slots])
            nc.vector.tensor_copy(f2[:].indirect(list4[:, entries]), w[:, slots])

        turned_sb = []
        for n in range(T // N_OUT):
            for b in range(N_OUT // P):
                nc.tensor.matmul(
                    turned[n][:, b * P : (b + 1) * P],
                    lhsT=f1[:, n * N_OUT + b * P : n * N_OUT + (b + 1) * P],
                    rhs=ident[:],
                    is_transpose=True,
                    start=False,
                    stop=(b == N_OUT // P - 1),
                )
            moved = keep.tile([P, N_OUT], F32, name="moved%d" % n)
            nc.scalar.copy(out=moved[:], in_=turned[n][:])
            turned_sb.append(moved)

        for n in range(T // N_OUT):
            cols = slice(n * N_OUT, (n + 1) * N_OUT)
            part = psum.tile([P, N_OUT], F32, name="part%d" % n, tag="bank%d" % (4 + n))
            for b in range(N_OUT // P):
                nc.tensor.transpose(part[:, b * P : (b + 1) * P], turned_sb[n][:, b * P : (b + 1) * P], ident[:])
            res = keep.tile([P, N_OUT], F32, name="res%d" % n)
            nc.vector.scalar_tensor_tensor(res[:], f2[:, cols], share_sb[:], part[:], ALU.mult, ALU.add)
            queue = nc.sync if n % 2 == 0 else nc.scalar
            queue.dma_start(out=out[:, cols], in_=res[:])
